import numpy as np
import ml_dtypes

BF16 = ml_dtypes.bfloat16


def bf(x):
    return np.asarray(x, np.float32).astype(BF16)


def f32(x):
    return np.asarray(x, np.float32)


def f64(x):
    return np.asarray(x).astype(np.float64)


def striped(idx):
    return np.tile(idx.reshape(-1, 16).T, (8, 1))


S, K, M, N = 512, 128, 512, 512


def setup_inputs():
    return {"table": bf(np.random.standard_normal((K, S))), "w": bf(np.random.standard_normal((K, M)) / np.sqrt(K)), "s": f32(0.5 + np.random.random_sample((M, 1))), "b": f32(0.5 * np.random.standard_normal((M, 1))), "offs": striped(np.random.permutation(S))}


def reference(table, w, s, b, offs):
    idx = offs[:16].T.reshape(-1)
    x = f64(table)[:, idx]
    y = f64(w).T @ x
    return y * f64(s) + f64(b)

@@ -1,0 +1,55 @@
+import concourse.mybir as mybir
+
+BF16, F32, U16 = mybir.dt.bfloat16, mybir.dt.float32, mybir.dt.uint16
+MULT, ADD = mybir.AluOpType.mult, mybir.AluOpType.add
+IDENTITY = mybir.ActivationFunctionType.Identity
+
+P = 128
+S = 512
+M = 512
+N = 512
+BLOCKS = M // P
+
+FLOPS = 2 * P * M * N
+
+
+def tile_gather_matmul_kernel(tc, table, w, s, b, offs, out):
+    nc = tc.nc
+    with (
+        tc.tile_pool(name="held", bufs=1) as held,
+        tc.tile_pool(name="staged", bufs=BLOCKS) as staged,
+        tc.psum_pool(name="psum", bufs=BLOCKS) as psum,
+    ):
+        offsets = held.tile([P, N // 16], U16, name="offsets")
+        nc.sync.dma_start(offsets[:], offs)
+        tokens = held.tile([P, S], BF16, name="tokens")
+        nc.scalar.dma_start(tokens[:], table)
+        weights = held.tile([P, M], BF16, name="weights")
+        nc.gpsimd.dma_start(weights[:], w)
+
+        gain = held.tile([P, BLOCKS], F32, name="gain")
+        shift = held.tile([P, BLOCKS], F32, name="shift")
+        with nc.allow_non_contiguous_dma(reason="one float32 to a partition for each block"):
+            nc.sync.dma_start(gain[:], s.rearrange("(a p) o -> p (a o)", p=P))
+            nc.scalar.dma_start(shift[:], b.rearrange("(a p) o -> p (a o)", p=P))
+
+        for a in range(BLOCKS):
+            bank = psum.tile([P, N], F32, name="bank")
+            nc.tensor.matmul(
+                bank[:],
+                weights[:, a * P : (a + 1) * P],
+                tokens[:].indirect(offsets[:]),
+                start=True,
+                stop=True,
+            )
+            result = staged.tile([P, N], F32, name="result")
+            if a % 2 == 0:
+                nc.vector.tensor_scalar(
+                    result[:], bank[:], gain[:, a : a + 1], shift[:, a : a + 1], MULT, ADD
+                )
+                nc.sync.dma_start(out[a * P : (a + 1) * P, :], result[:])
+            else:
+                nc.scalar.activation(
+                    result[:], bank[:], IDENTITY, bias=shift[:, a : a + 1], scale=gain[:, a : a + 1]
+                )
+                nc.scalar.dma_start(out[a * P : (a + 1) * P, :], result[:])

@@ -25,7 +25,7 @@ def tile_gather_matmul_kernel(tc, table, w, s, b, offs, out):
         tokens = held.tile([P, S], BF16, name="tokens")
         nc.scalar.dma_start(tokens[:], table)
         weights = held.tile([P, M], BF16, name="weights")
-        nc.gpsimd.dma_start(weights[:], w)
+        nc.sync.dma_start(weights[:], w)
 
         gain = held.tile([P, BLOCKS], F32, name="gain")
         shift = held.tile([P, BLOCKS], F32, name="shift")

@@ -9,6 +9,7 @@ S = 512
 M = 512
 N = 512
 BLOCKS = M // P
+WARMUPS = 3
 
 FLOPS = 2 * P * M * N
 
@@ -19,6 +20,7 @@ def tile_gather_matmul_kernel(tc, table, w, s, b, offs, out):
         tc.tile_pool(name="held", bufs=1) as held,
         tc.tile_pool(name="staged", bufs=BLOCKS) as staged,
         tc.psum_pool(name="psum", bufs=BLOCKS) as psum,
+        tc.psum_pool(name="spare", bufs=1) as spare,
     ):
         offsets = held.tile([P, N // 16], U16, name="offsets")
         nc.sync.dma_start(offsets[:], offs)
@@ -32,6 +34,12 @@ def tile_gather_matmul_kernel(tc, table, w, s, b, offs, out):
         with nc.allow_non_contiguous_dma(reason="one float32 to a partition for each block"):
             nc.sync.dma_start(gain[:], s.rearrange("(a p) o -> p (a o)", p=P))
             nc.scalar.dma_start(shift[:], b.rearrange("(a p) o -> p (a o)", p=P))
+
+        zeros = held.tile([P, N], BF16, name="zeros")
+        nc.vector.memset(zeros[:], 0.0)
+        unread = spare.tile([P, N], F32, name="unread")
+        for i in range(WARMUPS):
+            nc.tensor.matmul(unread[:], zeros[:, 0:P], zeros[:], start=True, stop=True)
 
         for a in range(BLOCKS):
             bank = psum.tile([P, N], F32, name="bank")

@@ -9,7 +9,6 @@ S = 512
 M = 512
 N = 512
 BLOCKS = M // P
-WARMUPS = 3
 
 FLOPS = 2 * P * M * N
 
@@ -20,7 +19,6 @@ def tile_gather_matmul_kernel(tc, table, w, s, b, offs, out):
         tc.tile_pool(name="held", bufs=1) as held,
         tc.tile_pool(name="staged", bufs=BLOCKS) as staged,
         tc.psum_pool(name="psum", bufs=BLOCKS) as psum,
-        tc.psum_pool(name="spare", bufs=1) as spare,
     ):
         offsets = held.tile([P, N // 16], U16, name="offsets")
         nc.sync.dma_start(offsets[:], offs)
@@ -35,11 +33,9 @@ def tile_gather_matmul_kernel(tc, table, w, s, b, offs, out):
             nc.sync.dma_start(gain[:], s.rearrange("(a p) o -> p (a o)", p=P))
             nc.scalar.dma_start(shift[:], b.rearrange("(a p) o -> p (a o)", p=P))
 
-        zeros = held.tile([P, N], BF16, name="zeros")
-        nc.vector.memset(zeros[:], 0.0)
-        unread = spare.tile([P, N], F32, name="unread")
-        for i in range(WARMUPS):
-            nc.tensor.matmul(unread[:], zeros[:, 0:P], zeros[:], start=True, stop=True)
+        primer = held.tile([P, 1], F32, name="primer")
+        nc.vector.memset(primer[:], 0.0)
+        nc.scalar.activation(primer[:], primer[:], IDENTITY)
 
         for a in range(BLOCKS):
             bank = psum.tile([P, N], F32, name="bank")

@@ -9,6 +9,8 @@ S = 512
 M = 512
 N = 512
 BLOCKS = M // P
+HALF = N // 2
+HALF_OFFSETS = HALF // 16
 
 FLOPS = 2 * P * M * N
 
@@ -17,8 +19,8 @@ def tile_gather_matmul_kernel(tc, table, w, s, b, offs, out):
     nc = tc.nc
     with (
         tc.tile_pool(name="held", bufs=1) as held,
-        tc.tile_pool(name="staged", bufs=BLOCKS) as staged,
-        tc.psum_pool(name="psum", bufs=BLOCKS) as psum,
+        tc.tile_pool(name="staged", bufs=2 * BLOCKS) as staged,
+        tc.psum_pool(name="psum", bufs=2 * BLOCKS) as psum,
     ):
         offsets = held.tile([P, N // 16], U16, name="offsets")
         nc.sync.dma_start(offsets[:], offs)
@@ -38,22 +40,25 @@ def tile_gather_matmul_kernel(tc, table, w, s, b, offs, out):
         nc.scalar.activation(primer[:], primer[:], IDENTITY)
 
         for a in range(BLOCKS):
-            bank = psum.tile([P, N], F32, name="bank")
-            nc.tensor.matmul(
-                bank[:],
-                weights[:, a * P : (a + 1) * P],
-                tokens[:].indirect(offsets[:]),
-                start=True,
-                stop=True,
-            )
-            result = staged.tile([P, N], F32, name="result")
-            if a % 2 == 0:
-                nc.vector.tensor_scalar(
-                    result[:], bank[:], gain[:, a : a + 1], shift[:, a : a + 1], MULT, ADD
+            features = slice(a * P, (a + 1) * P)
+            for h in range(2):
+                entries = slice(h * HALF, (h + 1) * HALF)
+                bank = psum.tile([P, HALF], F32, name="bank")
+                nc.tensor.matmul(
+                    bank[:],
+                    weights[:, features],
+                    tokens[:].indirect(offsets[:, h * HALF_OFFSETS : (h + 1) * HALF_OFFSETS]),
+                    start=True,
+                    stop=True,
                 )
-                nc.sync.dma_start(out[a * P : (a + 1) * P, :], result[:])
-            else:
-                nc.scalar.activation(
-                    result[:], bank[:], IDENTITY, bias=shift[:, a : a + 1], scale=gain[:, a : a + 1]
-                )
-                nc.scalar.dma_start(out[a * P : (a + 1) * P, :], result[:])
+                result = staged.tile([P, HALF], F32, name="result")
+                if h == 0:
+                    nc.vector.tensor_scalar(
+                        result[:], bank[:], gain[:, a : a + 1], shift[:, a : a + 1], MULT, ADD
+                    )
+                    nc.sync.dma_start(out[features, entries], result[:])
+                else:
+                    nc.scalar.activation(
+                        result[:], bank[:], IDENTITY, bias=shift[:, a : a + 1], scale=gain[:, a : a + 1]
+                    )
+                    nc.scalar.dma_start(out[features, entries], result[:])

@@ -11,6 +11,8 @@ N = 512
 BLOCKS = M // P
 HALF = N // 2
 HALF_OFFSETS = HALF // 16
+LOADS_OF_W = 2
+BLOCKS_A_LOAD = BLOCKS // LOADS_OF_W
 
 FLOPS = 2 * P * M * N
 
@@ -26,14 +28,15 @@ def tile_gather_matmul_kernel(tc, table, w, s, b, offs, out):
         nc.sync.dma_start(offsets[:], offs)
         tokens = held.tile([P, S], BF16, name="tokens")
         nc.scalar.dma_start(tokens[:], table)
-        weights = held.tile([P, M], BF16, name="weights")
-        nc.sync.dma_start(weights[:], w)
+        weights = [held.tile([P, BLOCKS_A_LOAD * P], BF16, name=f"weights{g}") for g in range(LOADS_OF_W)]
+        nc.sync.dma_start(weights[0][:], w[:, 0 : BLOCKS_A_LOAD * P])
+        nc.scalar.dma_start(weights[1][:], w[:, BLOCKS_A_LOAD * P : M])
 
         gain = held.tile([P, BLOCKS], F32, name="gain")
         shift = held.tile([P, BLOCKS], F32, name="shift")
         with nc.allow_non_contiguous_dma(reason="one float32 to a partition for each block"):
             nc.sync.dma_start(gain[:], s.rearrange("(a p) o -> p (a o)", p=P))
-            nc.scalar.dma_start(shift[:], b.rearrange("(a p) o -> p (a o)", p=P))
+            nc.sync.dma_start(shift[:], b.rearrange("(a p) o -> p (a o)", p=P))
 
         primer = held.tile([P, 1], F32, name="primer")
         nc.vector.memset(primer[:], 0.0)
@@ -41,12 +44,13 @@ def tile_gather_matmul_kernel(tc, table, w, s, b, offs, out):
 
         for a in range(BLOCKS):
             features = slice(a * P, (a + 1) * P)
+            block_of_w = weights[a // BLOCKS_A_LOAD][:, (a % BLOCKS_A_LOAD) * P : (a % BLOCKS_A_LOAD + 1) * P]
             for h in range(2):
                 entries = slice(h * HALF, (h + 1) * HALF)
                 bank = psum.tile([P, HALF], F32, name="bank")
                 nc.tensor.matmul(
                     bank[:],
-                    weights[:, features],
+                    block_of_w,
                     tokens[:].indirect(offsets[:, h * HALF_OFFSETS : (h + 1) * HALF_OFFSETS]),
                     start=True,
                     stop=True,

@@ -21,7 +21,7 @@ def tile_gather_matmul_kernel(tc, table, w, s, b, offs, out):
     nc = tc.nc
     with (
         tc.tile_pool(name="held", bufs=1) as held,
-        tc.tile_pool(name="staged", bufs=2 * BLOCKS) as staged,
+        tc.tile_pool(name="staged", bufs=BLOCKS) as staged,
         tc.psum_pool(name="psum", bufs=2 * BLOCKS) as psum,
     ):
         offsets = held.tile([P, N // 16], U16, name="offsets")
@@ -45,6 +45,7 @@ def tile_gather_matmul_kernel(tc, table, w, s, b, offs, out):
         for a in range(BLOCKS):
             features = slice(a * P, (a + 1) * P)
             block_of_w = weights[a // BLOCKS_A_LOAD][:, (a % BLOCKS_A_LOAD) * P : (a % BLOCKS_A_LOAD + 1) * P]
+            result = staged.tile([P, N], F32, name="result")
             for h in range(2):
                 entries = slice(h * HALF, (h + 1) * HALF)
                 bank = psum.tile([P, HALF], F32, name="bank")
@@ -55,14 +56,12 @@ def tile_gather_matmul_kernel(tc, table, w, s, b, offs, out):
                     start=True,
                     stop=True,
                 )
-                result = staged.tile([P, HALF], F32, name="result")
                 if h == 0:
                     nc.vector.tensor_scalar(
-                        result[:], bank[:], gain[:, a : a + 1], shift[:, a : a + 1], MULT, ADD
+                        result[:, entries], bank[:], gain[:, a : a + 1], shift[:, a : a + 1], MULT, ADD
                     )
-                    nc.sync.dma_start(out[features, entries], result[:])
                 else:
                     nc.scalar.activation(
-                        result[:], bank[:], IDENTITY, bias=shift[:, a : a + 1], scale=gain[:, a : a + 1]
+                        result[:, entries], bank[:], IDENTITY, bias=shift[:, a : a + 1], scale=gain[:, a : a + 1]
                     )
-                    nc.scalar.dma_start(out[features, entries], result[:])
+            nc.sync.dma_start(out[features, :], result[:])

@@ -30,13 +30,12 @@ def tile_gather_matmul_kernel(tc, table, w, s, b, offs, out):
         nc.scalar.dma_start(tokens[:], table)
         weights = [held.tile([P, BLOCKS_A_LOAD * P], BF16, name=f"weights{g}") for g in range(LOADS_OF_W)]
         nc.sync.dma_start(weights[0][:], w[:, 0 : BLOCKS_A_LOAD * P])
-        nc.scalar.dma_start(weights[1][:], w[:, BLOCKS_A_LOAD * P : M])
-
         gain = held.tile([P, BLOCKS], F32, name="gain")
         shift = held.tile([P, BLOCKS], F32, name="shift")
         with nc.allow_non_contiguous_dma(reason="one float32 to a partition for each block"):
             nc.sync.dma_start(gain[:], s.rearrange("(a p) o -> p (a o)", p=P))
-            nc.sync.dma_start(shift[:], b.rearrange("(a p) o -> p (a o)", p=P))
+            nc.scalar.dma_start(shift[:], b.rearrange("(a p) o -> p (a o)", p=P))
+        nc.scalar.dma_start(weights[1][:], w[:, BLOCKS_A_LOAD * P : M])
 
         primer = held.tile([P, 1], F32, name="primer")
         nc.vector.memset(primer[:], 0.0)

@@ -13,6 +13,8 @@ HALF = N // 2
 HALF_OFFSETS = HALF // 16
 LOADS_OF_W = 2
 BLOCKS_A_LOAD = BLOCKS // LOADS_OF_W
+PSUM_BANKS = 8
+WARM_UPS = 5
 
 FLOPS = 2 * P * M * N
 
@@ -22,7 +24,8 @@ def tile_gather_matmul_kernel(tc, table, w, s, b, offs, out):
     with (
         tc.tile_pool(name="held", bufs=1) as held,
         tc.tile_pool(name="staged", bufs=BLOCKS) as staged,
-        tc.psum_pool(name="psum", bufs=2 * BLOCKS) as psum,
+        tc.psum_pool(name="spare", bufs=1) as spare,
+        tc.psum_pool(name="psum", bufs=PSUM_BANKS - 1) as psum,
     ):
         offsets = held.tile([P, N // 16], U16, name="offsets")
         nc.sync.dma_start(offsets[:], offs)
@@ -40,6 +43,12 @@ def tile_gather_matmul_kernel(tc, table, w, s, b, offs, out):
         primer = held.tile([P, 1], F32, name="primer")
         nc.vector.memset(primer[:], 0.0)
         nc.scalar.activation(primer[:], primer[:], IDENTITY)
+
+        zeros = held.tile([P, HALF], BF16, name="zeros")
+        nc.vector.memset(zeros[:], 0.0)
+        unread = spare.tile([P, HALF], F32, name="unread")
+        for turn in range(WARM_UPS):
+            nc.tensor.matmul(unread[:], zeros[:, 0:P], zeros[:], start=True, stop=True)
 
         for a in range(BLOCKS):
             features = slice(a * P, (a + 1) * P)

@@ -11,8 +11,6 @@ N = 512
 BLOCKS = M // P
 HALF = N // 2
 HALF_OFFSETS = HALF // 16
-LOADS_OF_W = 2
-BLOCKS_A_LOAD = BLOCKS // LOADS_OF_W
 PSUM_BANKS = 8
 WARM_UPS = 5
 
@@ -31,14 +29,12 @@ def tile_gather_matmul_kernel(tc, table, w, s, b, offs, out):
         nc.sync.dma_start(offsets[:], offs)
         tokens = held.tile([P, S], BF16, name="tokens")
         nc.scalar.dma_start(tokens[:], table)
-        weights = [held.tile([P, BLOCKS_A_LOAD * P], BF16, name=f"weights{g}") for g in range(LOADS_OF_W)]
-        nc.sync.dma_start(weights[0][:], w[:, 0 : BLOCKS_A_LOAD * P])
+        weights = held.tile([P, M], BF16, name="weights")
+        nc.sync.dma_start(weights[:], w)
         gain = held.tile([P, BLOCKS], F32, name="gain")
+        nc.scalar.dma_start(gain[:], s.rearrange("(p a) o -> p (a o)", p=P))
         shift = held.tile([P, BLOCKS], F32, name="shift")
-        with nc.allow_non_contiguous_dma(reason="one float32 to a partition for each block"):
-            nc.sync.dma_start(gain[:], s.rearrange("(a p) o -> p (a o)", p=P))
-            nc.scalar.dma_start(shift[:], b.rearrange("(a p) o -> p (a o)", p=P))
-        nc.scalar.dma_start(weights[1][:], w[:, BLOCKS_A_LOAD * P : M])
+        nc.scalar.dma_start(shift[:], b.rearrange("(p a) o -> p (a o)", p=P))
 
         primer = held.tile([P, 1], F32, name="primer")
         nc.vector.memset(primer[:], 0.0)
@@ -50,9 +46,9 @@ def tile_gather_matmul_kernel(tc, table, w, s, b, offs, out):
         for turn in range(WARM_UPS):
             nc.tensor.matmul(unread[:], zeros[:, 0:P], zeros[:], start=True, stop=True)
 
+        rows = out.rearrange("(p a) n -> p a n", p=P)
         for a in range(BLOCKS):
-            features = slice(a * P, (a + 1) * P)
-            block_of_w = weights[a // BLOCKS_A_LOAD][:, (a % BLOCKS_A_LOAD) * P : (a % BLOCKS_A_LOAD + 1) * P]
+            block_of_w = weights[:, a:M:BLOCKS]
             result = staged.tile([P, N], F32, name="result")
             for h in range(2):
                 entries = slice(h * HALF, (h + 1) * HALF)
@@ -72,4 +68,4 @@ def tile_gather_matmul_kernel(tc, table, w, s, b, offs, out):
                     nc.scalar.activation(
                         result[:, entries], bank[:], IDENTITY, bias=shift[:, a : a + 1], scale=gain[:, a : a + 1]
                     )
-            nc.sync.dma_start(out[features, :], result[:])
+            nc.sync.dma_start(rows[:, a, :], result[:])

@@ -9,8 +9,10 @@ S = 512
 M = 512
 N = 512
 BLOCKS = M // P
-HALF = N // 2
-HALF_OFFSETS = HALF // 16
+PER_COLUMN = 16
+HALVES = (0, N // 2, N)
+SHORT_END = (0, 3 * N // 8, 3 * N // 4, N)
+WARM_COLUMNS = 256
 PSUM_BANKS = 8
 WARM_UPS = 5
 
@@ -40,32 +42,34 @@ def tile_gather_matmul_kernel(tc, table, w, s, b, offs, out):
         nc.vector.memset(primer[:], 0.0)
         nc.scalar.activation(primer[:], primer[:], IDENTITY)
 
-        zeros = held.tile([P, HALF], BF16, name="zeros")
+        zeros = held.tile([P, WARM_COLUMNS], BF16, name="zeros")
         nc.vector.memset(zeros[:], 0.0)
-        unread = spare.tile([P, HALF], F32, name="unread")
+        unread = spare.tile([P, WARM_COLUMNS], F32, name="unread")
         for turn in range(WARM_UPS):
             nc.tensor.matmul(unread[:], zeros[:, 0:P], zeros[:], start=True, stop=True)
 
         rows = out.rearrange("(p a) n -> p a n", p=P)
+        vectors_turn = True
         for a in range(BLOCKS):
             block_of_w = weights[:, a:M:BLOCKS]
             result = staged.tile([P, N], F32, name="result")
-            for h in range(2):
-                entries = slice(h * HALF, (h + 1) * HALF)
-                bank = psum.tile([P, HALF], F32, name="bank")
+            cuts = SHORT_END if a in (0, BLOCKS - 1) else HALVES
+            for first, end in zip(cuts[:-1], cuts[1:]):
+                bank = psum.tile([P, end - first], F32, name="bank")
                 nc.tensor.matmul(
                     bank[:],
                     block_of_w,
-                    tokens[:].indirect(offsets[:, h * HALF_OFFSETS : (h + 1) * HALF_OFFSETS]),
+                    tokens[:].indirect(offsets[:, first // PER_COLUMN : end // PER_COLUMN]),
                     start=True,
                     stop=True,
                 )
-                if h == 0:
+                if vectors_turn:
                     nc.vector.tensor_scalar(
-                        result[:, entries], bank[:], gain[:, a : a + 1], shift[:, a : a + 1], MULT, ADD
+                        result[:, first:end], bank[:], gain[:, a : a + 1], shift[:, a : a + 1], MULT, ADD
                     )
                 else:
                     nc.scalar.activation(
-                        result[:, entries], bank[:], IDENTITY, bias=shift[:, a : a + 1], scale=gain[:, a : a + 1]
+                        result[:, first:end], bank[:], IDENTITY, bias=shift[:, a : a + 1], scale=gain[:, a : a + 1]
                     )
+                vectors_turn = not vectors_turn
             nc.sync.dma_start(rows[:, a, :], result[:])

@@ -27,14 +27,14 @@ def tile_gather_matmul_kernel(tc, table, w, s, b, offs, out):
         tc.psum_pool(name="spare", bufs=1) as spare,
         tc.psum_pool(name="psum", bufs=PSUM_BANKS - 1) as psum,
     ):
-        offsets = held.tile([P, N // 16], U16, name="offsets")
-        nc.sync.dma_start(offsets[:], offs)
         tokens = held.tile([P, S], BF16, name="tokens")
         nc.scalar.dma_start(tokens[:], table)
         weights = held.tile([P, M], BF16, name="weights")
         nc.sync.dma_start(weights[:], w)
+        offsets = held.tile([P, N // PER_COLUMN], U16, name="offsets")
+        nc.sync.dma_start(offsets[:], offs)
         gain = held.tile([P, BLOCKS], F32, name="gain")
-        nc.scalar.dma_start(gain[:], s.rearrange("(p a) o -> p (a o)", p=P))
+        nc.sync.dma_start(gain[:], s.rearrange("(p a) o -> p (a o)", p=P))
         shift = held.tile([P, BLOCKS], F32, name="shift")
         nc.scalar.dma_start(shift[:], b.rearrange("(p a) o -> p (a o)", p=P))
 

@@ -10,8 +10,8 @@ M = 512
 N = 512
 BLOCKS = M // P
 PER_COLUMN = 16
-HALVES = (0, N // 2, N)
-SHORT_END = (0, 3 * N // 8, 3 * N // 4, N)
+HALF = N // 2
+QUARTER = N // 4
 WARM_COLUMNS = 256
 PSUM_BANKS = 8
 WARM_UPS = 5
@@ -49,13 +49,14 @@ def tile_gather_matmul_kernel(tc, table, w, s, b, offs, out):
             nc.tensor.matmul(unread[:], zeros[:, 0:P], zeros[:], start=True, stop=True)
 
         rows = out.rearrange("(p a) n -> p a n", p=P)
-        vectors_turn = True
         for a in range(BLOCKS):
             block_of_w = weights[:, a:M:BLOCKS]
             result = staged.tile([P, N], F32, name="result")
-            cuts = SHORT_END if a in (0, BLOCKS - 1) else HALVES
-            for first, end in zip(cuts[:-1], cuts[1:]):
-                bank = psum.tile([P, end - first], F32, name="bank")
+            at_an_edge = a in (0, BLOCKS - 1)
+            width = QUARTER if at_an_edge else HALF
+            for piece in range(N // width):
+                first, end = piece * width, (piece + 1) * width
+                bank = psum.tile([P, width], F32, name="bank")
                 nc.tensor.matmul(
                     bank[:],
                     block_of_w,
@@ -63,7 +64,7 @@ def tile_gather_matmul_kernel(tc, table, w, s, b, offs, out):
                     start=True,
                     stop=True,
                 )
-                if vectors_turn:
+                if piece % 2 == 0:
                     nc.vector.tensor_scalar(
                         result[:, first:end], bank[:], gain[:, a : a + 1], shift[:, a : a + 1], MULT, ADD
                     )
@@ -71,5 +72,7 @@ def tile_gather_matmul_kernel(tc, table, w, s, b, offs, out):
                     nc.scalar.activation(
                         result[:, first:end], bank[:], IDENTITY, bias=shift[:, a : a + 1], scale=gain[:, a : a + 1]
                     )
-                vectors_turn = not vectors_turn
-            nc.sync.dma_start(rows[:, a, :], result[:])
+                if at_an_edge and end % HALF == 0:
+                    nc.sync.dma_start(rows[:, a, end - HALF : end], result[:, end - HALF : end])
+            if not at_an_edge:
+                nc.sync.dma_start(rows[:, a, :], result[:])

@@ -53,10 +53,9 @@ def tile_gather_matmul_kernel(tc, table, w, s, b, offs, out):
             block_of_w = weights[:, a:M:BLOCKS]
             result = staged.tile([P, N], F32, name="result")
             at_an_edge = a in (0, BLOCKS - 1)
-            width = QUARTER if at_an_edge else HALF
-            for piece in range(N // width):
-                first, end = piece * width, (piece + 1) * width
-                bank = psum.tile([P, width], F32, name="bank")
+            for piece in range(N // QUARTER):
+                first, end = piece * QUARTER, (piece + 1) * QUARTER
+                bank = psum.tile([P, QUARTER], F32, name="bank")
                 nc.tensor.matmul(
                     bank[:],
                     block_of_w,

import concourse.mybir as mybir

BF16, F32, U16 = mybir.dt.bfloat16, mybir.dt.float32, mybir.dt.uint16
MULT, ADD = mybir.AluOpType.mult, mybir.AluOpType.add
IDENTITY = mybir.ActivationFunctionType.Identity

P = 128
S = 512
M = 512
N = 512
BLOCKS = M // P
PER_COLUMN = 16
HALF = N // 2
QUARTER = N // 4
WARM_COLUMNS = 256
PSUM_BANKS = 8
WARM_UPS = 5

FLOPS = 2 * P * M * N


def tile_gather_matmul_kernel(tc, table, w, s, b, offs, out):
    nc = tc.nc
    with (
        tc.tile_pool(name="held", bufs=1) as held,
        tc.tile_pool(name="staged", bufs=BLOCKS) as staged,
        tc.psum_pool(name="spare", bufs=1) as spare,
        tc.psum_pool(name="psum", bufs=PSUM_BANKS - 1) as psum,
    ):
        tokens = held.tile([P, S], BF16, name="tokens")
        nc.scalar.dma_start(tokens[:], table)
        weights = held.tile([P, M], BF16, name="weights")
        nc.sync.dma_start(weights[:], w)
        offsets = held.tile([P, N // PER_COLUMN], U16, name="offsets")
        nc.sync.dma_start(offsets[:], offs)
        gain = held.tile([P, BLOCKS], F32, name="gain")
        nc.sync.dma_start(gain[:], s.rearrange("(p a) o -> p (a o)", p=P))
        shift = held.tile([P, BLOCKS], F32, name="shift")
        nc.scalar.dma_start(shift[:], b.rearrange("(p a) o -> p (a o)", p=P))

        primer = held.tile([P, 1], F32, name="primer")
        nc.vector.memset(primer[:], 0.0)
        nc.scalar.activation(primer[:], primer[:], IDENTITY)

        zeros = held.tile([P, WARM_COLUMNS], BF16, name="zeros")
        nc.vector.memset(zeros[:], 0.0)
        unread = spare.tile([P, WARM_COLUMNS], F32, name="unread")
        for turn in range(WARM_UPS):
            nc.tensor.matmul(unread[:], zeros[:, 0:P], zeros[:], start=True, stop=True)

        rows = out.rearrange("(p a) n -> p a n", p=P)
        for a in range(BLOCKS):
            block_of_w = weights[:, a:M:BLOCKS]
            result = staged.tile([P, N], F32, name="result")
            at_an_edge = a in (0, BLOCKS - 1)
            for piece in range(N // QUARTER):
                first, end = piece * QUARTER, (piece + 1) * QUARTER
                bank = psum.tile([P, QUARTER], F32, name="bank")
                nc.tensor.matmul(
                    bank[:],
                    block_of_w,
                    tokens[:].indirect(offsets[:, first // PER_COLUMN : end // PER_COLUMN]),
                    start=True,
                    stop=True,
                )
                if piece % 2 == 0:
                    nc.vector.tensor_scalar(
                        result[:, first:end], bank[:], gain[:, a : a + 1], shift[:, a : a + 1], MULT, ADD
                    )
                else:
                    nc.scalar.activation(
                        result[:, first:end], bank[:], IDENTITY, bias=shift[:, a : a + 1], scale=gain[:, a : a + 1]
                    )
                if at_an_edge and end % HALF == 0:
                    nc.sync.dma_start(rows[:, a, end - HALF : end], result[:, end - HALF : end])
            if not at_an_edge:
                nc.sync.dma_start(rows[:, a, :], result[:])
